import numpy as np
import ml_dtypes


def mxq(x, axis, fmt="e4m3"):
    dtype, down = {"e4m3": (ml_dtypes.float8_e4m3fn, 7), "e5m2": (ml_dtypes.float8_e5m2, 14)}[fmt]
    v = np.moveaxis(np.asarray(x, np.float32).astype(ml_dtypes.bfloat16).astype(np.float64), axis, -1)
    blocks = v.reshape(v.shape[:-1] + (-1, 32))
    amax = np.abs(blocks).max(-1, keepdims=True)
    byte = np.maximum(np.where(amax > 0, np.frexp(amax)[1] - 1 + 127, 0) - down, 1)
    scale = np.exp2(byte - 127.0)
    codes = (blocks / scale).astype(np.float32).astype(dtype).astype(np.float64)
    return np.moveaxis((codes * scale).reshape(v.shape), -1, axis)


WIDE = False


def mx_kscale(k):
    if not WIDE:
        return np.ones(k)
    levels = np.array([10, -10, 5, -5, 0])
    if k % 512:
        return np.exp2(np.random.permutation(np.resize(levels, k // 32))).repeat(32)
    a = np.empty((k // 512, 16))
    for p in range(k // 512):
        a[p, :8] = np.random.permutation(np.resize(levels, 8))
        for g in range(8):
            far = levels[np.abs(levels - a[p, g]) >= 10]
            a[p, g + 8] = far[np.random.randint(len(far))]
    return np.exp2(a.ravel()).repeat(32)


def f64(x):
    return np.asarray(x).astype(np.float64)


def striped(idx):
    return np.tile(np.asarray(idx).reshape(-1, 16).T, (8, 1)).astype(np.uint16)


def unstriped(offs):
    return offs[:16].T.reshape(-1).astype(np.int64)


def striped8(idx):
    return np.asarray(idx).reshape(8, -1, 16).transpose(0, 2, 1).reshape(128, -1).astype(np.uint16)


def unstriped8(offs):
    return offs.reshape(8, 16, -1).transpose(0, 2, 1).reshape(8, -1).astype(np.int64)


def pick8(x, idx, run):
    r = np.arange(len(x))
    return x[r[:, None], idx[r % (8 * run) // run]]


E2M1 = np.array([0.0, 0.5, 1.0, 1.5, 2.0, 3.0, 4.0, 6.0, -0.0, -0.5, -1.0, -1.5, -2.0, -3.0, -4.0, -6.0])


def pack_weight(w, fmt):
    k, n = w.shape
    w = f64(np.asarray(w, np.float32).astype(ml_dtypes.bfloat16)).reshape(k // 32, 32, n)
    amax = np.abs(w).max(1)
    if fmt == "e4m3":
        byte = np.frexp(amax)[1] - 1 + 127 - 7
    else:
        mant, ex = np.frexp(amax / 6.0)
        byte = np.where(mant > 0.5, ex, ex - 1) + 127
    byte = np.clip(np.where(amax > 0, byte, 1), 1, 254)
    scaled = (w * np.exp2(127.0 - byte)[:, None, :]).reshape(k, n).astype(np.float32)
    by_word = np.ascontiguousarray(scaled.reshape(k // 512, 128, 4, n).transpose(0, 1, 3, 2))
    if fmt == "e4m3":
        words = by_word.astype(ml_dtypes.float8_e4m3fn).view(np.uint8)
    else:
        c = by_word.astype(ml_dtypes.float4_e2m1fn).view(np.uint8) & 0xF
        words = (c[..., 0::2] | (c[..., 1::2] << 4)).reshape(k // 512, 128, 2 * n)
    return np.ascontiguousarray(words), np.ascontiguousarray(byte.astype(np.uint8).reshape(k // 512, 16, n))


def unpack_weight(words, scales, fmt):
    g, _, n = scales.shape
    words = np.ascontiguousarray(words).reshape(g, 128, n, -1)
    if fmt == "e4m3":
        vals = words.view(ml_dtypes.float8_e4m3fn).astype(np.float64)
    else:
        nib = np.empty((g, 128, n, 4), np.uint8)
        nib[..., 0::2] = words & 0xF
        nib[..., 1::2] = words >> 4
        vals = E2M1[nib]
    vals = vals * np.repeat(np.exp2(scales.astype(np.float64) - 127.0), 8, axis=1)[..., None]
    return vals.transpose(0, 1, 3, 2).reshape(g * 512, n)


K, J, R, T, U, Z, M, O, C, N = 512, 256, 512, 1024, 512, 512, 1024, 128, 512, 256


def setup_inputs():
    n = np.random.standard_normal
    idx = np.stack([np.random.permutation(T)[:U] for _ in range(8)])
    idx2 = np.random.permutation(U)[:J]
    idx3 = np.stack([np.random.permutation(U)[:J] for _ in range(8)])
    idx4 = np.random.permutation(M)[:J]
    idx5 = np.stack([np.random.permutation(C)[:J] for _ in range(8)])
    idx6 = np.stack([np.random.permutation(C)[:O] for _ in range(8)])
    idx7 = np.stack([np.random.permutation(J)[:O] for _ in range(8)])
    fk = mx_kscale(K)
    fr = mx_kscale(R)
    fz = mx_kscale(Z)
    wp = pack_weight(n((K, R)) * 1 / np.sqrt(K) / fk[:, None] * fr, "e2m1")
    xop = pack_weight(n((Z, M)) / fz[:, None], "e2m1")
    w2p = pack_weight(n((Z, R)) * 1 / np.sqrt(Z) * fz[:, None] * fr, "e4m3")
    wbp = pack_weight(n((R, N)) * 1 / np.sqrt(R) / fr[:, None], "e4m3")
    return {
        "ta": (np.random.randint(-7, 8, (K, T)).astype(np.float64)).astype(np.float32),
        "ga": ((np.random.randint(8, 25, (K, 1)) / 64.0) * fk[:, None]).astype(np.float32),
        "gb": (np.random.uniform(0.5, 1.6, (K, 1))).astype(np.float32),
        "gd": (np.random.uniform(0.5, 1.6, (K, 1))).astype(np.float32),
        "w_words": wp[0],
        "w_scales": wp[1],
        "xo_words": xop[0],
        "xo_scales": xop[1],
        "w2_words": w2p[0],
        "w2_scales": w2p[1],
        "sa": (np.random.uniform(0.5, 1.6, (R, 1))).astype(np.float32),
        "sb": (np.random.uniform(0.5, 1.6, (R, 1))).astype(np.float32),
        "wb_words": wbp[0],
        "wb_scales": wbp[1],
        "offs": striped8(idx),
        "offs2": striped(idx2),
        "offs3": striped8(idx3),
        "offs4": striped(idx4),
        "offs5": striped8(idx5),
        "offs6": striped8(idx6),
        "offs7": striped8(idx7),
    }


def reference(ta, ga, gb, gd, w_words, w_scales, xo_words, xo_scales, w2_words, w2_scales, sa, sb, wb_words, wb_scales, offs, offs2, offs3, offs4, offs5, offs6, offs7):
    idx = unstriped8(offs)
    idx2 = unstriped(offs2)
    idx3 = unstriped8(offs3)
    idx4 = unstriped(offs4)
    idx5 = unstriped8(offs5)
    idx6 = unstriped8(offs6)
    idx7 = unstriped8(offs7)
    wu = unpack_weight(w_words, w_scales, "e2m1")
    xou = unpack_weight(xo_words, xo_scales, "e2m1")
    w2u = unpack_weight(w2_words, w2_scales, "e4m3")
    wbu = unpack_weight(wb_words, wb_scales, "e4m3")
    xcd = pick8(f64(ta), idx, 64) * f64(ga)
    xc = np.maximum(xcd[:, idx2] * f64(gb), pick8(xcd, idx3, 64) * f64(gd))
    xcq = mxq(xc, 0, "e4m3")
    a = wu.T @ xcq
    xoidx4g = xou[:, idx4]
    b = w2u.T @ xoidx4g
    pw = np.zeros((R, C))
    pw[np.arange(R)[:, None], idx5[np.arange(R) % 512 // 64]] = a
    hid = np.maximum(pick8(pw, idx6, 64) * f64(sa), pick8(b, idx7, 64) * f64(sb))
    hidq = mxq(hid, 0, "e4m3")
    y = wbu.T @ hidq
    return y

@@ -1,0 +1,239 @@
+from contextlib import ExitStack
+
+import concourse.mybir as mybir
+
+K, J, R, T, U, Z, M, O, C, N = 512, 256, 512, 1024, 512, 512, 1024, 128, 512, 256
+FLOPS = 2 * K * R * J + 2 * Z * R * J + 2 * R * N * O
+
+F32 = mybir.dt.float32
+BF16 = mybir.dt.bfloat16
+I32 = mybir.dt.int32
+U32 = mybir.dt.uint32
+U16 = mybir.dt.uint16
+U8 = mybir.dt.uint8
+FP8X4 = mybir.dt.float8_e4m3fn_x4
+FP4X4 = mybir.dt.float4_e2m1fn_x4
+COPY = mybir.ActivationFunctionType.Copy
+MAX = mybir.AluOpType.max
+
+P = 128
+PACK = 4
+QUADS = 4
+HALF = J // 2
+ALIGN = 64
+LINE = 4
+
+
+def tile_picked_crossspelled_plain_two_boardmeet_one_plain_kernel(
+    tc, ta, ga, gb, gd, w_words, w_scales, xo_words, xo_scales, w2_words, w2_scales, sa, sb,
+    wb_words, wb_scales, offs, offs2, offs3, offs4, offs5, offs6, offs7, out,
+):
+    nc = tc.nc
+    with ExitStack() as ctx:
+        lists = ctx.enter_context(tc.tile_pool(name="lists", bufs=1))
+        sb_pool = ctx.enter_context(tc.tile_pool(name="work", bufs=1))
+        psum = ctx.enter_context(tc.psum_pool(name="psum", bufs=1))
+
+        def tile(name, shape, dtype, tag=None):
+            return sb_pool.tile(shape, dtype, name=name, tag=tag or name, align_bytes=ALIGN)
+
+        def load_list(name, src):
+            dst = lists.tile(list(src.shape), U16, name=name, tag=name)
+            nc.sync.dma_start(dst[:], src)
+            return dst
+
+        def load_gain(name, src, queue):
+            dst = tile(name, [P, PACK], F32)
+            queue.dma_start(dst[:], src.rearrange("(p t) o -> p (t o)", t=PACK))
+            return dst
+
+        def scale_rows(src):
+            return src[0].bitcast(I32).rearrange("(q r) n -> r q n", r=4)
+
+        def gather(dst, window, offsets, gain):
+            nc.scalar.activation(out=dst, in_=window[:].indirect(offsets), func=COPY, scale=gain)
+
+        def larger(dst, t0, t1, first, second):
+            if t1 - t0 == 1:
+                view = dst[:].rearrange("p (j t) -> p t j", t=PACK)[:, t0, :]
+                nc.vector.tensor_tensor(view, first, second, MAX)
+            else:
+                view = dst[:].rearrange("p (c i t) -> p c t i", i=LINE, t=PACK)[:, :, t0:t1, :]
+                order = "p t (c i) -> p c t i"
+                nc.vector.tensor_tensor(view, first.rearrange(order, i=LINE), second.rearrange(order, i=LINE), MAX)
+
+        def quantize(name, src):
+            codes = tile(name + "_codes", [P, HALF], U32)
+            scales = tile(name + "_scales", [P, HALF], U8)
+            nc.vector.quantize_mx(out=codes[:].bitcast(FP8X4), scales=scales[:], in_=src[:])
+            return codes, scales
+
+        w_raw_s = tile("w_raw_s", [P, QUADS, R], U8)
+        w2_raw_s = tile("w2_raw_s", [P, QUADS, R], U8)
+        xo_s = tile("xo_s", [P, M], U8)
+        wb_s = tile("wb_s", [P, N], U8)
+        nc.vector.memset(w_raw_s[:, 0, :].bitcast(I32), 0)
+        nc.vector.memset(w2_raw_s[:, 0, :].bitcast(I32), 0)
+        nc.vector.memset(xo_s[:].bitcast(I32), 0)
+        nc.vector.memset(wb_s[:].bitcast(I32), 0)
+        pw = [tile("pw%d" % t, [P, C], F32) for t in range(PACK)]
+        for t in range(PACK):
+            nc.vector.memset(pw[t][:], 0.0)
+
+        ta_rows = ta.rearrange("(p t) c -> t p c", t=PACK)
+        ta_sb = [tile("ta%d" % t, [P, T], F32) for t in range(PACK)]
+        nc.sync.dma_start(ta_sb[0][:], ta_rows[0])
+        ga_sb = load_gain("ga", ga, nc.scalar)
+        gb_sb = load_gain("gb", gb, nc.scalar)
+        gd_sb = load_gain("gd", gd, nc.scalar)
+        l1 = load_list("l1", offs)
+        l2 = load_list("l2", offs2)
+        l3 = load_list("l3", offs3)
+        nc.sync.dma_start(ta_sb[1][:], ta_rows[1])
+        nc.sync.dma_start(w_raw_s[0:4].bitcast(I32), scale_rows(w_scales))
+        w_raw = tile("w_raw", [P, 2 * R], U8)
+        nc.sync.dma_start(w_raw[:].bitcast(I32), w_words[0].bitcast(I32))
+        xo_stage = tile("xo_stage", [4, QUADS, M // 4], I32)
+        nc.sync.dma_start(xo_stage[:], scale_rows(xo_scales))
+        l4 = load_list("l4", offs4)
+        xo_w = tile("xo_w", [P, M], U16)
+        nc.sync.dma_start(xo_w[:].bitcast(I32), xo_words[0].bitcast(I32))
+        nc.sync.dma_start(ta_sb[2][:], ta_rows[2])
+        nc.sync.dma_start(w2_raw_s[0:4].bitcast(I32), scale_rows(w2_scales))
+        w2_raw = tile("w2_raw", [P, R], I32)
+        nc.sync.dma_start(w2_raw[:], w2_words[0].rearrange("p n t -> p (n t)").bitcast(I32))
+        nc.sync.dma_start(ta_sb[3][:], ta_rows[3])
+        l5 = load_list("l5", offs5)
+        wb_w = tile("wb_w", [P, N], I32)
+        nc.sync.dma_start(wb_w[:], wb_words[0].rearrange("p n t -> p (n t)").bitcast(I32))
+        l6 = load_list("l6", offs6)
+        l7 = load_list("l7", offs7)
+        sa_sb = load_gain("sa", sa, nc.sync)
+        sb_sb = load_gain("sb", sb, nc.sync)
+        wb_rows = wb_scales[0].bitcast(I32)
+        for q in range(QUADS):
+            nc.sync.dma_start(wb_s[32 * q : 32 * q + 4, :].bitcast(I32), wb_rows[4 * q : 4 * q + 4, :])
+
+        def deal_scales(name, raw):
+            words = raw[:].bitcast(I32)
+            for q in range(1, QUADS):
+                nc.vector.tensor_copy(words[32 * q : 32 * q + 4, 0, :], words[0:4, q, :])
+            dealt = tile(name, [P, R], U8)
+            nc.vector.tensor_copy(
+                dealt[:].rearrange("p (t m) -> p m t", t=PACK), raw[:, 0, :].rearrange("p (m t) -> p m t", t=PACK)
+            )
+            return dealt
+
+        w_s = deal_scales("w_s", w_raw_s)
+        w_w = tile("w_w", [P, 2 * R], U8)
+        nc.vector.tensor_copy(
+            w_w[:].rearrange("p (t m b) -> p m t b", t=PACK, b=2), w_raw[:].rearrange("p (m t b) -> p m t b", t=PACK, b=2)
+        )
+
+        xo_s_words = xo_s[:].bitcast(I32)
+        for q in range(QUADS):
+            nc.vector.tensor_copy(xo_s_words[32 * q : 32 * q + 4, :], xo_stage[:, q, :])
+        xg_w = tile("xg_w", [P, J], U16)
+        xg_s = tile("xg_s", [P, J], U8)
+        nc.vector.tensor_copy(xg_w[:], xo_w[:].indirect(l4[:]))
+        nc.vector.tensor_copy(xg_s[:], xo_s[:].indirect(l4[:]))
+
+        w2_s = deal_scales("w2_s", w2_raw_s)
+        w2_w = tile("w2_w", [P, R], I32)
+        nc.vector.tensor_copy(
+            w2_w[:].rearrange("p (t m) -> p m t", t=PACK), w2_raw[:].rearrange("p (m t) -> p m t", t=PACK)
+        )
+
+        b_ps = [psum.tile([P, 2, J], F32, name="b_ps%d" % g) for g in range(2)]
+        for t in range(PACK):
+            cols = slice(t * P, (t + 1) * P)
+            nc.tensor.matmul_mx(
+                out=b_ps[t // 2][:, t % 2, :], lhsT=w2_w[:, cols].bitcast(FP8X4), lhsT_scale=w2_s[:, cols],
+                rhs=xg_w[:].bitcast(FP4X4), rhs_scale=xg_s[:], start=True, stop=True,
+            )
+
+        def first_product(dst, t, codes, scales):
+            nc.tensor.matmul_mx(
+                out=dst, lhsT=w_w[:, 2 * t * P : 2 * (t + 1) * P].bitcast(FP4X4), lhsT_scale=w_s[:, t * P : (t + 1) * P],
+                rhs=codes[:].bitcast(FP8X4), rhs_scale=scales[:], start=True, stop=True,
+            )
+
+        def half_list(lst, h):
+            return lst[:, h * (HALF // 16) : (h + 1) * (HALF // 16)]
+
+        xcd = [tile("xcd%d" % t, [P, U], F32) for t in range(PACK)]
+        g0a = tile("g0a", [P, 2, PACK - 1, HALF], F32)
+        g0b = tile("g0b", [P, 2, HALF], F32)
+        for t in range(PACK):
+            gather(xcd[t][:], ta_sb[t], l1[:], ga_sb[:, t : t + 1])
+            for i, (lst, gain) in enumerate(((l2, gb_sb), (l3, gd_sb))):
+                dst = g0a[:, i, t, :] if t < PACK - 1 else g0b[:, i, :]
+                gather(dst, xcd[t], half_list(lst, 0), gain[:, t : t + 1])
+        xc0 = tile("xc0", [P, PACK * HALF], BF16)
+        larger(xc0, 0, PACK - 1, g0a[:, 0], g0a[:, 1])
+        larger(xc0, PACK - 1, PACK, g0b[:, 0, :], g0b[:, 1, :])
+        x0_c, x0_s = quantize("x0", xc0)
+        a0_ps = [psum.tile([P, 2, HALF], F32, name="a0_ps%d" % g) for g in range(2)]
+        for t in range(PACK):
+            first_product(a0_ps[t // 2][:, t % 2, :], t, x0_c, x0_s)
+
+        g1 = tile("g1", [P, 2, PACK, HALF], F32, tag="ta3")
+        for t in range(PACK):
+            for i, (lst, gain) in enumerate(((l2, gb_sb), (l3, gd_sb))):
+                gather(g1[:, i, t, :], xcd[t], half_list(lst, 1), gain[:, t : t + 1])
+
+        a0a = tile("a0a", [P, 2, HALF], F32)
+        nc.vector.tensor_copy(a0a[:], a0_ps[0][:])
+        for t in range(2):
+            nc.vector.tensor_copy(pw[t][:].indirect(half_list(l5, 0)), a0a[:, t, :])
+
+        xc1 = tile("xc1", [P, PACK * HALF], BF16, tag="a0a")
+        larger(xc1, 0, PACK, g1[:, 0], g1[:, 1])
+        x1_c, x1_s = quantize("x1", xc1)
+
+        a0b = tile("a0b", [P, 2, HALF], F32, tag="ta3")
+        nc.scalar.copy(a0b[:], a0_ps[1][:])
+        for t in range(2, PACK):
+            nc.vector.tensor_copy(pw[t][:].indirect(half_list(l5, 0)), a0b[:, t - 2, :])
+
+        a1_ps0 = psum.tile([P, HALF], F32, name="a1_ps0")
+        a1_ps1 = psum.tile([P, PACK - 1, HALF], F32, name="a1_ps1")
+        first_product(a1_ps0[:], 0, x1_c, x1_s)
+        for t in range(1, PACK):
+            first_product(a1_ps1[:, t - 1, :], t, x1_c, x1_s)
+        a1a = tile("a1a", [P, HALF], F32)
+        a1b = tile("a1b", [P, PACK - 1, HALF], F32)
+        nc.scalar.copy(a1a[:], a1_ps0[:])
+        nc.scalar.copy(a1b[:], a1_ps1[:])
+
+        b_sb = [tile("b%d" % t, [P, J], F32, tag="xcd%d" % t) for t in range(PACK)]
+        for t in range(PACK):
+            nc.scalar.copy(b_sb[t][:], b_ps[t // 2][:, t % 2, :])
+
+        for t in range(PACK):
+            src = a1a[:] if t == 0 else a1b[:, t - 1, :]
+            nc.vector.tensor_copy(pw[t][:].indirect(half_list(l5, 1)), src)
+
+        pga = tile("pga", [P, PACK - 1, O], F32)
+        pgb = tile("pgb", [P, O], F32)
+        bg = tile("bg", [P, PACK, O], F32, tag="a1a")
+        for t in range(PACK):
+            dst = pga[:, t, :] if t < PACK - 1 else pgb[:]
+            gather(dst, pw[t], l6[:], sa_sb[:, t : t + 1])
+        for t in range(PACK):
+            gather(bg[:, t, :], b_sb[t], l7[:], sb_sb[:, t : t + 1])
+        hid = tile("hid", [P, PACK * O], BF16)
+        larger(hid, 0, PACK - 1, pga[:], bg[:, 0 : PACK - 1, :])
+        larger(hid, PACK - 1, PACK, pgb[:], bg[:, PACK - 1, :])
+        h_c, h_s = quantize("hid", hid)
+
+        for g, (copy, queue) in enumerate(((nc.vector.tensor_copy, nc.sync), (nc.scalar.copy, nc.scalar))):
+            cols = slice(g * P, (g + 1) * P)
+            y_ps = psum.tile([P, O], F32, name="y_ps%d" % g)
+            nc.tensor.matmul_mx(
+                out=y_ps[:], lhsT=wb_w[:, cols].bitcast(FP8X4), lhsT_scale=wb_s[:, cols],
+                rhs=h_c[:].bitcast(FP8X4), rhs_scale=h_s[:], start=True, stop=True,
+            )
+            y = tile("y%d" % g, [P, O], F32)
+            copy(y[:], y_ps[:])
+            queue.dma_start(out[cols, :], y[:])

@@ -21,7 +21,7 @@ PACK = 4
 QUADS = 4
 HALF = J // 2
 ALIGN = 64
-LINE = 4
+LINE = 2
 
 
 def tile_picked_crossspelled_plain_two_boardmeet_one_plain_kernel(
@@ -32,10 +32,14 @@ def tile_picked_crossspelled_plain_two_boardmeet_one_plain_kernel(
     with ExitStack() as ctx:
         lists = ctx.enter_context(tc.tile_pool(name="lists", bufs=1))
         sb_pool = ctx.enter_context(tc.tile_pool(name="work", bufs=1))
+        ring = ctx.enter_context(tc.tile_pool(name="ring", bufs=1))
         psum = ctx.enter_context(tc.psum_pool(name="psum", bufs=1))
 
         def tile(name, shape, dtype, tag=None):
             return sb_pool.tile(shape, dtype, name=name, tag=tag or name, align_bytes=ALIGN)
+
+        def placed(name, shape, offset):
+            return ring.tile(shape, F32, name=name, tag=name, offset=offset)
 
         def load_list(name, src):
             dst = lists.tile(list(src.shape), U16, name=name, tag=name)
@@ -47,8 +51,15 @@ def tile_picked_crossspelled_plain_two_boardmeet_one_plain_kernel(
             queue.dma_start(dst[:], src.rearrange("(p t) o -> p (t o)", t=PACK))
             return dst
 
-        def scale_rows(src):
-            return src[0].bitcast(I32).rearrange("(q r) n -> r q n", r=4)
+        def load_scales(plane, src):
+            rows = src[0].bitcast(I32)
+            for q in range(QUADS):
+                nc.sync.dma_start(plane[32 * q : 32 * q + 4, :].bitcast(I32), rows[4 * q : 4 * q + 4, :])
+
+        def stage_scales(raw, src):
+            rows = src[0].bitcast(I32).rearrange("(u q r) n -> u r q n", u=2, r=4)
+            for u in range(2):
+                nc.sync.dma_start(raw[64 * u : 64 * u + 4].bitcast(I32), rows[u])
 
         def gather(dst, window, offsets, gain):
             nc.scalar.activation(out=dst, in_=window[:].indirect(offsets), func=COPY, scale=gain)
@@ -68,8 +79,8 @@ def tile_picked_crossspelled_plain_two_boardmeet_one_plain_kernel(
             nc.vector.quantize_mx(out=codes[:].bitcast(FP8X4), scales=scales[:], in_=src[:])
             return codes, scales
 
-        w_raw_s = tile("w_raw_s", [P, QUADS, R], U8)
-        w2_raw_s = tile("w2_raw_s", [P, QUADS, R], U8)
+        w_raw_s = tile("w_raw_s", [P, 2, R], U8)
+        w2_raw_s = tile("w2_raw_s", [P, 2, R], U8)
         xo_s = tile("xo_s", [P, M], U8)
         wb_s = tile("wb_s", [P, N], U8)
         nc.vector.memset(w_raw_s[:, 0, :].bitcast(I32), 0)
@@ -81,28 +92,27 @@ def tile_picked_crossspelled_plain_two_boardmeet_one_plain_kernel(
             nc.vector.memset(pw[t][:], 0.0)
 
         ta_rows = ta.rearrange("(p t) c -> t p c", t=PACK)
-        ta_sb = [tile("ta%d" % t, [P, T], F32) for t in range(PACK)]
+        ta_sb = [placed("ta%d" % t, [P, T], 4 * T * t) for t in range(PACK)]
         nc.sync.dma_start(ta_sb[0][:], ta_rows[0])
-        ga_sb = load_gain("ga", ga, nc.scalar)
-        gb_sb = load_gain("gb", gb, nc.scalar)
-        gd_sb = load_gain("gd", gd, nc.scalar)
+        ga_sb = load_gain("ga", ga, nc.sync)
+        gb_sb = load_gain("gb", gb, nc.gpsimd)
+        gd_sb = load_gain("gd", gd, nc.gpsimd)
         l1 = load_list("l1", offs)
+        nc.sync.dma_start(ta_sb[1][:], ta_rows[1])
         l2 = load_list("l2", offs2)
         l3 = load_list("l3", offs3)
-        nc.sync.dma_start(ta_sb[1][:], ta_rows[1])
-        nc.sync.dma_start(w_raw_s[0:4].bitcast(I32), scale_rows(w_scales))
+        stage_scales(w_raw_s, w_scales)
         w_raw = tile("w_raw", [P, 2 * R], U8)
         nc.sync.dma_start(w_raw[:].bitcast(I32), w_words[0].bitcast(I32))
-        xo_stage = tile("xo_stage", [4, QUADS, M // 4], I32)
-        nc.sync.dma_start(xo_stage[:], scale_rows(xo_scales))
+        nc.sync.dma_start(ta_sb[2][:], ta_rows[2])
         l4 = load_list("l4", offs4)
         xo_w = tile("xo_w", [P, M], U16)
         nc.sync.dma_start(xo_w[:].bitcast(I32), xo_words[0].bitcast(I32))
-        nc.sync.dma_start(ta_sb[2][:], ta_rows[2])
-        nc.sync.dma_start(w2_raw_s[0:4].bitcast(I32), scale_rows(w2_scales))
+        load_scales(xo_s, xo_scales)
+        nc.sync.dma_start(ta_sb[3][:], ta_rows[3])
+        stage_scales(w2_raw_s, w2_scales)
         w2_raw = tile("w2_raw", [P, R], I32)
         nc.sync.dma_start(w2_raw[:], w2_words[0].rearrange("p n t -> p (n t)").bitcast(I32))
-        nc.sync.dma_start(ta_sb[3][:], ta_rows[3])
         l5 = load_list("l5", offs5)
         wb_w = tile("wb_w", [P, N], I32)
         nc.sync.dma_start(wb_w[:], wb_words[0].rearrange("p n t -> p (n t)").bitcast(I32))
@@ -110,47 +120,30 @@ def tile_picked_crossspelled_plain_two_boardmeet_one_plain_kernel(
         l7 = load_list("l7", offs7)
         sa_sb = load_gain("sa", sa, nc.sync)
         sb_sb = load_gain("sb", sb, nc.sync)
-        wb_rows = wb_scales[0].bitcast(I32)
-        for q in range(QUADS):
-            nc.sync.dma_start(wb_s[32 * q : 32 * q + 4, :].bitcast(I32), wb_rows[4 * q : 4 * q + 4, :])
+        load_scales(wb_s, wb_scales)
 
         def deal_scales(name, raw):
             words = raw[:].bitcast(I32)
-            for q in range(1, QUADS):
-                nc.vector.tensor_copy(words[32 * q : 32 * q + 4, 0, :], words[0:4, q, :])
+            for u in range(2):
+                nc.vector.tensor_copy(words[64 * u + 32 : 64 * u + 36, 0, :], words[64 * u : 64 * u + 4, 1, :])
             dealt = tile(name, [P, R], U8)
             nc.vector.tensor_copy(
-                dealt[:].rearrange("p (t m) -> p m t", t=PACK), raw[:, 0, :].rearrange("p (m t) -> p m t", t=PACK)
+                dealt[:].rearrange("p (t m) -> p t m", t=PACK), raw[:, 0, :].rearrange("p (m t) -> p t m", t=PACK)
             )
             return dealt
 
         w_s = deal_scales("w_s", w_raw_s)
         w_w = tile("w_w", [P, 2 * R], U8)
         nc.vector.tensor_copy(
-            w_w[:].rearrange("p (t m b) -> p m t b", t=PACK, b=2), w_raw[:].rearrange("p (m t b) -> p m t b", t=PACK, b=2)
+            w_w[:].rearrange("p (t m b) -> p t m b", t=PACK, b=2), w_raw[:].rearrange("p (m t b) -> p t m b", t=PACK, b=2)
         )
 
-        xo_s_words = xo_s[:].bitcast(I32)
-        for q in range(QUADS):
-            nc.vector.tensor_copy(xo_s_words[32 * q : 32 * q + 4, :], xo_stage[:, q, :])
         xg_w = tile("xg_w", [P, J], U16)
         xg_s = tile("xg_s", [P, J], U8)
         nc.vector.tensor_copy(xg_w[:], xo_w[:].indirect(l4[:]))
         nc.vector.tensor_copy(xg_s[:], xo_s[:].indirect(l4[:]))
 
         w2_s = deal_scales("w2_s", w2_raw_s)
-        w2_w = tile("w2_w", [P, R], I32)
-        nc.vector.tensor_copy(
-            w2_w[:].rearrange("p (t m) -> p m t", t=PACK), w2_raw[:].rearrange("p (m t) -> p m t", t=PACK)
-        )
-
-        b_ps = [psum.tile([P, 2, J], F32, name="b_ps%d" % g) for g in range(2)]
-        for t in range(PACK):
-            cols = slice(t * P, (t + 1) * P)
-            nc.tensor.matmul_mx(
-                out=b_ps[t // 2][:, t % 2, :], lhsT=w2_w[:, cols].bitcast(FP8X4), lhsT_scale=w2_s[:, cols],
-                rhs=xg_w[:].bitcast(FP4X4), rhs_scale=xg_s[:], start=True, stop=True,
-            )
 
         def first_product(dst, t, codes, scales):
             nc.tensor.matmul_mx(
@@ -162,22 +155,34 @@ def tile_picked_crossspelled_plain_two_boardmeet_one_plain_kernel(
             return lst[:, h * (HALF // 16) : (h + 1) * (HALF // 16)]
 
         xcd = [tile("xcd%d" % t, [P, U], F32) for t in range(PACK)]
-        g0a = tile("g0a", [P, 2, PACK - 1, HALF], F32)
-        g0b = tile("g0b", [P, 2, HALF], F32)
-        for t in range(PACK):
-            gather(xcd[t][:], ta_sb[t], l1[:], ga_sb[:, t : t + 1])
-            for i, (lst, gain) in enumerate(((l2, gb_sb), (l3, gd_sb))):
-                dst = g0a[:, i, t, :] if t < PACK - 1 else g0b[:, i, :]
-                gather(dst, xcd[t], half_list(lst, 0), gain[:, t : t + 1])
-        xc0 = tile("xc0", [P, PACK * HALF], BF16)
-        larger(xc0, 0, PACK - 1, g0a[:, 0], g0a[:, 1])
-        larger(xc0, PACK - 1, PACK, g0b[:, 0, :], g0b[:, 1, :])
+        g0 = [placed("g0_%d" % u, [P, 2, 2, HALF], 4 * T * (2 * u + 1)) for u in range(2)]
+        xc0 = tile("xc0", [P, PACK * HALF], BF16, tag="xo_w")
+        for u in range(2):
+            for t in range(2 * u, 2 * u + 2):
+                gather(xcd[t][:], ta_sb[t], l1[:], ga_sb[:, t : t + 1])
+            for t in range(2 * u, 2 * u + 2):
+                for i, (lst, gain) in enumerate(((l2, gb_sb), (l3, gd_sb))):
+                    gather(g0[u][:, i, t - 2 * u, :], xcd[t], half_list(lst, 0), gain[:, t : t + 1])
+            larger(xc0, 2 * u, 2 * u + 2, g0[u][:, 0], g0[u][:, 1])
         x0_c, x0_s = quantize("x0", xc0)
         a0_ps = [psum.tile([P, 2, HALF], F32, name="a0_ps%d" % g) for g in range(2)]
         for t in range(PACK):
             first_product(a0_ps[t // 2][:, t % 2, :], t, x0_c, x0_s)
 
-        g1 = tile("g1", [P, 2, PACK, HALF], F32, tag="ta3")
+        w2_w = tile("w2_w", [P, R], I32, tag="xo_w")
+        nc.vector.tensor_copy(
+            w2_w[:].rearrange("p (t c i) -> p c t i", t=PACK, i=4), w2_raw[:].rearrange("p (c i t) -> p c t i", t=PACK, i=4)
+        )
+
+        b_ps = [psum.tile([P, 2, J], F32, name="b_ps%d" % g) for g in range(2)]
+        for t in range(PACK):
+            cols = slice(t * P, (t + 1) * P)
+            nc.tensor.matmul_mx(
+                out=b_ps[t // 2][:, t % 2, :], lhsT=w2_w[:, cols].bitcast(FP8X4), lhsT_scale=w2_s[:, cols],
+                rhs=xg_w[:].bitcast(FP4X4), rhs_scale=xg_s[:], start=True, stop=True,
+            )
+
+        g1 = placed("g1", [P, 2, PACK, HALF], 4 * T * 3 + 2048)
         for t in range(PACK):
             for i, (lst, gain) in enumerate(((l2, gb_sb), (l3, gd_sb))):
                 gather(g1[:, i, t, :], xcd[t], half_list(lst, 1), gain[:, t : t + 1])
@@ -191,7 +196,7 @@ def tile_picked_crossspelled_plain_two_boardmeet_one_plain_kernel(
         larger(xc1, 0, PACK, g1[:, 0], g1[:, 1])
         x1_c, x1_s = quantize("x1", xc1)
 
-        a0b = tile("a0b", [P, 2, HALF], F32, tag="ta3")
+        a0b = placed("a0b", [P, 2, HALF], 4 * T * 4)
         nc.scalar.copy(a0b[:], a0_ps[1][:])
         for t in range(2, PACK):
             nc.vector.tensor_copy(pw[t][:].indirect(half_list(l5, 0)), a0b[:, t - 2, :])

@@ -21,7 +21,7 @@ PACK = 4
 QUADS = 4
 HALF = J // 2
 ALIGN = 64
-LINE = 2
+LINE = 4
 
 
 def tile_picked_crossspelled_plain_two_boardmeet_one_plain_kernel(
@@ -79,6 +79,9 @@ def tile_picked_crossspelled_plain_two_boardmeet_one_plain_kernel(
             nc.vector.quantize_mx(out=codes[:].bitcast(FP8X4), scales=scales[:], in_=src[:])
             return codes, scales
 
+        warm = tile("warm", [P, 2], F32)
+        nc.vector.memset(warm[:, 0:1], 0.0)
+        nc.scalar.activation(out=warm[:, 1:2], in_=warm[:, 0:1], func=COPY)
         w_raw_s = tile("w_raw_s", [P, 2, R], U8)
         w2_raw_s = tile("w2_raw_s", [P, 2, R], U8)
         xo_s = tile("xo_s", [P, M], U8)
@@ -94,25 +97,25 @@ def tile_picked_crossspelled_plain_two_boardmeet_one_plain_kernel(
         ta_rows = ta.rearrange("(p t) c -> t p c", t=PACK)
         ta_sb = [placed("ta%d" % t, [P, T], 4 * T * t) for t in range(PACK)]
         nc.sync.dma_start(ta_sb[0][:], ta_rows[0])
-        ga_sb = load_gain("ga", ga, nc.sync)
-        gb_sb = load_gain("gb", gb, nc.gpsimd)
-        gd_sb = load_gain("gd", gd, nc.gpsimd)
         l1 = load_list("l1", offs)
+        ga_sb = load_gain("ga", ga, nc.sync)
         nc.sync.dma_start(ta_sb[1][:], ta_rows[1])
+        gb_sb = load_gain("gb", gb, nc.sync)
+        gd_sb = load_gain("gd", gd, nc.sync)
+        stage_scales(w_raw_s, w_scales)
         l2 = load_list("l2", offs2)
         l3 = load_list("l3", offs3)
-        stage_scales(w_raw_s, w_scales)
+        nc.sync.dma_start(ta_sb[2][:], ta_rows[2])
         w_raw = tile("w_raw", [P, 2 * R], U8)
         nc.sync.dma_start(w_raw[:].bitcast(I32), w_words[0].bitcast(I32))
-        nc.sync.dma_start(ta_sb[2][:], ta_rows[2])
+        stage_scales(w2_raw_s, w2_scales)
         l4 = load_list("l4", offs4)
         xo_w = tile("xo_w", [P, M], U16)
         nc.sync.dma_start(xo_w[:].bitcast(I32), xo_words[0].bitcast(I32))
-        load_scales(xo_s, xo_scales)
         nc.sync.dma_start(ta_sb[3][:], ta_rows[3])
-        stage_scales(w2_raw_s, w2_scales)
         w2_raw = tile("w2_raw", [P, R], I32)
         nc.sync.dma_start(w2_raw[:], w2_words[0].rearrange("p n t -> p (n t)").bitcast(I32))
+        load_scales(xo_s, xo_scales)
         l5 = load_list("l5", offs5)
         wb_w = tile("wb_w", [P, N], I32)
         nc.sync.dma_start(wb_w[:], wb_words[0].rearrange("p n t -> p (n t)").bitcast(I32))
@@ -138,12 +141,23 @@ def tile_picked_crossspelled_plain_two_boardmeet_one_plain_kernel(
             w_w[:].rearrange("p (t m b) -> p t m b", t=PACK, b=2), w_raw[:].rearrange("p (m t b) -> p t m b", t=PACK, b=2)
         )
 
+        w2_s = deal_scales("w2_s", w2_raw_s)
         xg_w = tile("xg_w", [P, J], U16)
         xg_s = tile("xg_s", [P, J], U8)
         nc.vector.tensor_copy(xg_w[:], xo_w[:].indirect(l4[:]))
+        w2_w = tile("w2_w", [P, R], I32)
+        nc.vector.tensor_copy(
+            w2_w[:].rearrange("p (t c i) -> p c t i", t=PACK, i=4), w2_raw[:].rearrange("p (c i t) -> p c t i", t=PACK, i=4)
+        )
         nc.vector.tensor_copy(xg_s[:], xo_s[:].indirect(l4[:]))
 
-        w2_s = deal_scales("w2_s", w2_raw_s)
+        b_ps = [psum.tile([P, 2, J], F32, name="b_ps%d" % g, tag="bank%d" % g) for g in range(2)]
+        for t in range(PACK):
+            cols = slice(t * P, (t + 1) * P)
+            nc.tensor.matmul_mx(
+                out=b_ps[t // 2][:, t % 2, :], lhsT=w2_w[:, cols].bitcast(FP8X4), lhsT_scale=w2_s[:, cols],
+                rhs=xg_w[:].bitcast(FP4X4), rhs_scale=xg_s[:], start=True, stop=True,
+            )
 
         def first_product(dst, t, codes, scales):
             nc.tensor.matmul_mx(
@@ -156,48 +170,40 @@ def tile_picked_crossspelled_plain_two_boardmeet_one_plain_kernel(
 
         xcd = [tile("xcd%d" % t, [P, U], F32) for t in range(PACK)]
         g0 = [placed("g0_%d" % u, [P, 2, 2, HALF], 4 * T * (2 * u + 1)) for u in range(2)]
-        xc0 = tile("xc0", [P, PACK * HALF], BF16, tag="xo_w")
+        xc0 = tile("xc0", [P, PACK * HALF], BF16, tag="xo_s")
         for u in range(2):
             for t in range(2 * u, 2 * u + 2):
                 gather(xcd[t][:], ta_sb[t], l1[:], ga_sb[:, t : t + 1])
             for t in range(2 * u, 2 * u + 2):
                 for i, (lst, gain) in enumerate(((l2, gb_sb), (l3, gd_sb))):
                     gather(g0[u][:, i, t - 2 * u, :], xcd[t], half_list(lst, 0), gain[:, t : t + 1])
-            larger(xc0, 2 * u, 2 * u + 2, g0[u][:, 0], g0[u][:, 1])
+                if u == 1:
+                    larger(xc0, t, t + 1, g0[u][:, 0, t - 2, :], g0[u][:, 1, t - 2, :])
+            if u == 0:
+                larger(xc0, 0, 2, g0[u][:, 0], g0[u][:, 1])
         x0_c, x0_s = quantize("x0", xc0)
-        a0_ps = [psum.tile([P, 2, HALF], F32, name="a0_ps%d" % g) for g in range(2)]
+        a0_ps = [psum.tile([P, HALF], F32, name="a0_ps%d" % t) for t in range(2)]
+        a0_ps_b = psum.tile([P, 2, HALF], F32, name="a0_ps_b")
         for t in range(PACK):
-            first_product(a0_ps[t // 2][:, t % 2, :], t, x0_c, x0_s)
-
-        w2_w = tile("w2_w", [P, R], I32, tag="xo_w")
-        nc.vector.tensor_copy(
-            w2_w[:].rearrange("p (t c i) -> p c t i", t=PACK, i=4), w2_raw[:].rearrange("p (c i t) -> p c t i", t=PACK, i=4)
-        )
-
-        b_ps = [psum.tile([P, 2, J], F32, name="b_ps%d" % g) for g in range(2)]
-        for t in range(PACK):
-            cols = slice(t * P, (t + 1) * P)
-            nc.tensor.matmul_mx(
-                out=b_ps[t // 2][:, t % 2, :], lhsT=w2_w[:, cols].bitcast(FP8X4), lhsT_scale=w2_s[:, cols],
-                rhs=xg_w[:].bitcast(FP4X4), rhs_scale=xg_s[:], start=True, stop=True,
-            )
+            first_product(a0_ps[t][:] if t < 2 else a0_ps_b[:, t - 2, :], t, x0_c, x0_s)
 
         g1 = placed("g1", [P, 2, PACK, HALF], 4 * T * 3 + 2048)
         for t in range(PACK):
             for i, (lst, gain) in enumerate(((l2, gb_sb), (l3, gd_sb))):
                 gather(g1[:, i, t, :], xcd[t], half_list(lst, 1), gain[:, t : t + 1])
 
-        a0a = tile("a0a", [P, 2, HALF], F32)
-        nc.vector.tensor_copy(a0a[:], a0_ps[0][:])
+        a0a = [tile("a0a%d" % t, [P, HALF], F32) for t in range(2)]
         for t in range(2):
-            nc.vector.tensor_copy(pw[t][:].indirect(half_list(l5, 0)), a0a[:, t, :])
+            nc.vector.tensor_copy(a0a[t][:], a0_ps[t][:])
+        for t in range(2):
+            nc.vector.tensor_copy(pw[t][:].indirect(half_list(l5, 0)), a0a[t][:])
 
-        xc1 = tile("xc1", [P, PACK * HALF], BF16, tag="a0a")
+        xc1 = tile("xc1", [P, PACK * HALF], BF16, tag="a0a1")
         larger(xc1, 0, PACK, g1[:, 0], g1[:, 1])
         x1_c, x1_s = quantize("x1", xc1)
 
         a0b = placed("a0b", [P, 2, HALF], 4 * T * 4)
-        nc.scalar.copy(a0b[:], a0_ps[1][:])
+        nc.scalar.copy(a0b[:], a0_ps_b[:])
         for t in range(2, PACK):
             nc.vector.tensor_copy(pw[t][:].indirect(half_list(l5, 0)), a0b[:, t - 2, :])
 
@@ -234,7 +240,7 @@ def tile_picked_crossspelled_plain_two_boardmeet_one_plain_kernel(
 
         for g, (copy, queue) in enumerate(((nc.vector.tensor_copy, nc.sync), (nc.scalar.copy, nc.scalar))):
             cols = slice(g * P, (g + 1) * P)
-            y_ps = psum.tile([P, O], F32, name="y_ps%d" % g)
+            y_ps = psum.tile([P, O], F32, name="y_ps%d" % g, tag="bank%d" % g)
             nc.tensor.matmul_mx(
                 out=y_ps[:], lhsT=wb_w[:, cols].bitcast(FP8X4), lhsT_scale=wb_s[:, cols],
                 rhs=h_c[:].bitcast(FP8X4), rhs_scale=h_s[:], start=True, stop=True,

@@ -52,9 +52,9 @@ def tile_picked_crossspelled_plain_two_boardmeet_one_plain_kernel(
             return dst
 
         def load_scales(plane, src):
-            rows = src[0].bitcast(I32)
-            for q in range(QUADS):
-                nc.sync.dma_start(plane[32 * q : 32 * q + 4, :].bitcast(I32), rows[4 * q : 4 * q + 4, :])
+            rows = src[0].bitcast(I32).rearrange("(q r) n -> r q n", r=4)
+            for r in range(4):
+                nc.sync.dma_start(plane[r:P:32, :].bitcast(I32), rows[r])
 
         def stage_scales(raw, src):
             rows = src[0].bitcast(I32).rearrange("(u q r) n -> u r q n", u=2, r=4)
@@ -96,12 +96,12 @@ def tile_picked_crossspelled_plain_two_boardmeet_one_plain_kernel(
 
         ta_rows = ta.rearrange("(p t) c -> t p c", t=PACK)
         ta_sb = [placed("ta%d" % t, [P, T], 4 * T * t) for t in range(PACK)]
-        nc.sync.dma_start(ta_sb[0][:], ta_rows[0])
         l1 = load_list("l1", offs)
-        ga_sb = load_gain("ga", ga, nc.sync)
+        nc.sync.dma_start(ta_sb[0][:], ta_rows[0])
+        ga_sb = load_gain("ga", ga, nc.scalar)
         nc.sync.dma_start(ta_sb[1][:], ta_rows[1])
-        gb_sb = load_gain("gb", gb, nc.sync)
-        gd_sb = load_gain("gd", gd, nc.sync)
+        gb_sb = load_gain("gb", gb, nc.scalar)
+        gd_sb = load_gain("gd", gd, nc.scalar)
         stage_scales(w_raw_s, w_scales)
         l2 = load_list("l2", offs2)
         l3 = load_list("l3", offs3)
@@ -198,7 +198,7 @@ def tile_picked_crossspelled_plain_two_boardmeet_one_plain_kernel(
         for t in range(2):
             nc.vector.tensor_copy(pw[t][:].indirect(half_list(l5, 0)), a0a[t][:])
 
-        xc1 = tile("xc1", [P, PACK * HALF], BF16, tag="a0a1")
+        xc1 = tile("xc1", [P, PACK * HALF], BF16, tag="a0a0")
         larger(xc1, 0, PACK, g1[:, 0], g1[:, 1])
         x1_c, x1_s = quantize("x1", xc1)
 

from contextlib import ExitStack

import concourse.mybir as mybir

K, J, R, T, U, Z, M, O, C, N = 512, 256, 512, 1024, 512, 512, 1024, 128, 512, 256
FLOPS = 2 * K * R * J + 2 * Z * R * J + 2 * R * N * O

F32 = mybir.dt.float32
BF16 = mybir.dt.bfloat16
I32 = mybir.dt.int32
U32 = mybir.dt.uint32
U16 = mybir.dt.uint16
U8 = mybir.dt.uint8
FP8X4 = mybir.dt.float8_e4m3fn_x4
FP4X4 = mybir.dt.float4_e2m1fn_x4
COPY = mybir.ActivationFunctionType.Copy
MAX = mybir.AluOpType.max

P = 128
PACK = 4
QUADS = 4
HALF = J // 2
ALIGN = 64
LINE = 4


def tile_picked_crossspelled_plain_two_boardmeet_one_plain_kernel(
    tc, ta, ga, gb, gd, w_words, w_scales, xo_words, xo_scales, w2_words, w2_scales, sa, sb,
    wb_words, wb_scales, offs, offs2, offs3, offs4, offs5, offs6, offs7, out,
):
    nc = tc.nc
    with ExitStack() as ctx:
        lists = ctx.enter_context(tc.tile_pool(name="lists", bufs=1))
        sb_pool = ctx.enter_context(tc.tile_pool(name="work", bufs=1))
        ring = ctx.enter_context(tc.tile_pool(name="ring", bufs=1))
        psum = ctx.enter_context(tc.psum_pool(name="psum", bufs=1))

        def tile(name, shape, dtype, tag=None):
            return sb_pool.tile(shape, dtype, name=name, tag=tag or name, align_bytes=ALIGN)

        def placed(name, shape, offset):
            return ring.tile(shape, F32, name=name, tag=name, offset=offset)

        def load_list(name, src):
            dst = lists.tile(list(src.shape), U16, name=name, tag=name)
            nc.sync.dma_start(dst[:], src)
            return dst

        def load_gain(name, src, queue):
            dst = tile(name, [P, PACK], F32)
            queue.dma_start(dst[:], src.rearrange("(p t) o -> p (t o)", t=PACK))
            return dst

        def load_scales(plane, src):
            rows = src[0].bitcast(I32).rearrange("(q r) n -> r q n", r=4)
            for r in range(4):
                nc.sync.dma_start(plane[r:P:32, :].bitcast(I32), rows[r])

        def stage_scales(raw, src):
            rows = src[0].bitcast(I32).rearrange("(u q r) n -> u r q n", u=2, r=4)
            for u in range(2):
                nc.sync.dma_start(raw[64 * u : 64 * u + 4].bitcast(I32), rows[u])

        def gather(dst, window, offsets, gain):
            nc.scalar.activation(out=dst, in_=window[:].indirect(offsets), func=COPY, scale=gain)

        def larger(dst, t0, t1, first, second):
            if t1 - t0 == 1:
                view = dst[:].rearrange("p (j t) -> p t j", t=PACK)[:, t0, :]
                nc.vector.tensor_tensor(view, first, second, MAX)
            else:
                view = dst[:].rearrange("p (c i t) -> p c t i", i=LINE, t=PACK)[:, :, t0:t1, :]
                order = "p t (c i) -> p c t i"
                nc.vector.tensor_tensor(view, first.rearrange(order, i=LINE), second.rearrange(order, i=LINE), MAX)

        def quantize(name, src):
            codes = tile(name + "_codes", [P, HALF], U32)
            scales = tile(name + "_scales", [P, HALF], U8)
            nc.vector.quantize_mx(out=codes[:].bitcast(FP8X4), scales=scales[:], in_=src[:])
            return codes, scales

        warm = tile("warm", [P, 2], F32)
        nc.vector.memset(warm[:, 0:1], 0.0)
        nc.scalar.activation(out=warm[:, 1:2], in_=warm[:, 0:1], func=COPY)
        w_raw_s = tile("w_raw_s", [P, 2, R], U8)
        w2_raw_s = tile("w2_raw_s", [P, 2, R], U8)
        xo_s = tile("xo_s", [P, M], U8)
        wb_s = tile("wb_s", [P, N], U8)
        nc.vector.memset(w_raw_s[:, 0, :].bitcast(I32), 0)
        nc.vector.memset(w2_raw_s[:, 0, :].bitcast(I32), 0)
        nc.vector.memset(xo_s[:].bitcast(I32), 0)
        nc.vector.memset(wb_s[:].bitcast(I32), 0)
        pw = [tile("pw%d" % t, [P, C], F32) for t in range(PACK)]
        for t in range(PACK):
            nc.vector.memset(pw[t][:], 0.0)

        ta_rows = ta.rearrange("(p t) c -> t p c", t=PACK)
        ta_sb = [placed("ta%d" % t, [P, T], 4 * T * t) for t in range(PACK)]
        l1 = load_list("l1", offs)
        nc.sync.dma_start(ta_sb[0][:], ta_rows[0])
        ga_sb = load_gain("ga", ga, nc.scalar)
        nc.sync.dma_start(ta_sb[1][:], ta_rows[1])
        gb_sb = load_gain("gb", gb, nc.scalar)
        gd_sb = load_gain("gd", gd, nc.scalar)
        stage_scales(w_raw_s, w_scales)
        l2 = load_list("l2", offs2)
        l3 = load_list("l3", offs3)
        nc.sync.dma_start(ta_sb[2][:], ta_rows[2])
        w_raw = tile("w_raw", [P, 2 * R], U8)
        nc.sync.dma_start(w_raw[:].bitcast(I32), w_words[0].bitcast(I32))
        stage_scales(w2_raw_s, w2_scales)
        l4 = load_list("l4", offs4)
        xo_w = tile("xo_w", [P, M], U16)
        nc.sync.dma_start(xo_w[:].bitcast(I32), xo_words[0].bitcast(I32))
        nc.sync.dma_start(ta_sb[3][:], ta_rows[3])
        w2_raw = tile("w2_raw", [P, R], I32)
        nc.sync.dma_start(w2_raw[:], w2_words[0].rearrange("p n t -> p (n t)").bitcast(I32))
        load_scales(xo_s, xo_scales)
        l5 = load_list("l5", offs5)
        wb_w = tile("wb_w", [P, N], I32)
        nc.sync.dma_start(wb_w[:], wb_words[0].rearrange("p n t -> p (n t)").bitcast(I32))
        l6 = load_list("l6", offs6)
        l7 = load_list("l7", offs7)
        sa_sb = load_gain("sa", sa, nc.sync)
        sb_sb = load_gain("sb", sb, nc.sync)
        load_scales(wb_s, wb_scales)

        def deal_scales(name, raw):
            words = raw[:].bitcast(I32)
            for u in range(2):
                nc.vector.tensor_copy(words[64 * u + 32 : 64 * u + 36, 0, :], words[64 * u : 64 * u + 4, 1, :])
            dealt = tile(name, [P, R], U8)
            nc.vector.tensor_copy(
                dealt[:].rearrange("p (t m) -> p t m", t=PACK), raw[:, 0, :].rearrange("p (m t) -> p t m", t=PACK)
            )
            return dealt

        w_s = deal_scales("w_s", w_raw_s)
        w_w = tile("w_w", [P, 2 * R], U8)
        nc.vector.tensor_copy(
            w_w[:].rearrange("p (t m b) -> p t m b", t=PACK, b=2), w_raw[:].rearrange("p (m t b) -> p t m b", t=PACK, b=2)
        )

        w2_s = deal_scales("w2_s", w2_raw_s)
        xg_w = tile("xg_w", [P, J], U16)
        xg_s = tile("xg_s", [P, J], U8)
        nc.vector.tensor_copy(xg_w[:], xo_w[:].indirect(l4[:]))
        w2_w = tile("w2_w", [P, R], I32)
        nc.vector.tensor_copy(
            w2_w[:].rearrange("p (t c i) -> p c t i", t=PACK, i=4), w2_raw[:].rearrange("p (c i t) -> p c t i", t=PACK, i=4)
        )
        nc.vector.tensor_copy(xg_s[:], xo_s[:].indirect(l4[:]))

        b_ps = [psum.tile([P, 2, J], F32, name="b_ps%d" % g, tag="bank%d" % g) for g in range(2)]
        for t in range(PACK):
            cols = slice(t * P, (t + 1) * P)
            nc.tensor.matmul_mx(
                out=b_ps[t // 2][:, t % 2, :], lhsT=w2_w[:, cols].bitcast(FP8X4), lhsT_scale=w2_s[:, cols],
                rhs=xg_w[:].bitcast(FP4X4), rhs_scale=xg_s[:], start=True, stop=True,
            )

        def first_product(dst, t, codes, scales):
            nc.tensor.matmul_mx(
                out=dst, lhsT=w_w[:, 2 * t * P : 2 * (t + 1) * P].bitcast(FP4X4), lhsT_scale=w_s[:, t * P : (t + 1) * P],
                rhs=codes[:].bitcast(FP8X4), rhs_scale=scales[:], start=True, stop=True,
            )

        def half_list(lst, h):
            return lst[:, h * (HALF // 16) : (h + 1) * (HALF // 16)]

        xcd = [tile("xcd%d" % t, [P, U], F32) for t in range(PACK)]
        g0 = [placed("g0_%d" % u, [P, 2, 2, HALF], 4 * T * (2 * u + 1)) for u in range(2)]
        xc0 = tile("xc0", [P, PACK * HALF], BF16, tag="xo_s")
        for u in range(2):
            for t in range(2 * u, 2 * u + 2):
                gather(xcd[t][:], ta_sb[t], l1[:], ga_sb[:, t : t + 1])
            for t in range(2 * u, 2 * u + 2):
                for i, (lst, gain) in enumerate(((l2, gb_sb), (l3, gd_sb))):
                    gather(g0[u][:, i, t - 2 * u, :], xcd[t], half_list(lst, 0), gain[:, t : t + 1])
                if u == 1:
                    larger(xc0, t, t + 1, g0[u][:, 0, t - 2, :], g0[u][:, 1, t - 2, :])
            if u == 0:
                larger(xc0, 0, 2, g0[u][:, 0], g0[u][:, 1])
        x0_c, x0_s = quantize("x0", xc0)
        a0_ps = [psum.tile([P, HALF], F32, name="a0_ps%d" % t) for t in range(2)]
        a0_ps_b = psum.tile([P, 2, HALF], F32, name="a0_ps_b")
        for t in range(PACK):
            first_product(a0_ps[t][:] if t < 2 else a0_ps_b[:, t - 2, :], t, x0_c, x0_s)

        g1 = placed("g1", [P, 2, PACK, HALF], 4 * T * 3 + 2048)
        for t in range(PACK):
            for i, (lst, gain) in enumerate(((l2, gb_sb), (l3, gd_sb))):
                gather(g1[:, i, t, :], xcd[t], half_list(lst, 1), gain[:, t : t + 1])

        a0a = [tile("a0a%d" % t, [P, HALF], F32) for t in range(2)]
        for t in range(2):
            nc.vector.tensor_copy(a0a[t][:], a0_ps[t][:])
        for t in range(2):
            nc.vector.tensor_copy(pw[t][:].indirect(half_list(l5, 0)), a0a[t][:])

        xc1 = tile("xc1", [P, PACK * HALF], BF16, tag="a0a0")
        larger(xc1, 0, PACK, g1[:, 0], g1[:, 1])
        x1_c, x1_s = quantize("x1", xc1)

        a0b = placed("a0b", [P, 2, HALF], 4 * T * 4)
        nc.scalar.copy(a0b[:], a0_ps_b[:])
        for t in range(2, PACK):
            nc.vector.tensor_copy(pw[t][:].indirect(half_list(l5, 0)), a0b[:, t - 2, :])

        a1_ps0 = psum.tile([P, HALF], F32, name="a1_ps0")
        a1_ps1 = psum.tile([P, PACK - 1, HALF], F32, name="a1_ps1")
        first_product(a1_ps0[:], 0, x1_c, x1_s)
        for t in range(1, PACK):
            first_product(a1_ps1[:, t - 1, :], t, x1_c, x1_s)
        a1a = tile("a1a", [P, HALF], F32)
        a1b = tile("a1b", [P, PACK - 1, HALF], F32)
        nc.scalar.copy(a1a[:], a1_ps0[:])
        nc.scalar.copy(a1b[:], a1_ps1[:])

        b_sb = [tile("b%d" % t, [P, J], F32, tag="xcd%d" % t) for t in range(PACK)]
        for t in range(PACK):
            nc.scalar.copy(b_sb[t][:], b_ps[t // 2][:, t % 2, :])

        for t in range(PACK):
            src = a1a[:] if t == 0 else a1b[:, t - 1, :]
            nc.vector.tensor_copy(pw[t][:].indirect(half_list(l5, 1)), src)

        pga = tile("pga", [P, PACK - 1, O], F32)
        pgb = tile("pgb", [P, O], F32)
        bg = tile("bg", [P, PACK, O], F32, tag="a1a")
        for t in range(PACK):
            dst = pga[:, t, :] if t < PACK - 1 else pgb[:]
            gather(dst, pw[t], l6[:], sa_sb[:, t : t + 1])
        for t in range(PACK):
            gather(bg[:, t, :], b_sb[t], l7[:], sb_sb[:, t : t + 1])
        hid = tile("hid", [P, PACK * O], BF16)
        larger(hid, 0, PACK - 1, pga[:], bg[:, 0 : PACK - 1, :])
        larger(hid, PACK - 1, PACK, pgb[:], bg[:, PACK - 1, :])
        h_c, h_s = quantize("hid", hid)

        for g, (copy, queue) in enumerate(((nc.vector.tensor_copy, nc.sync), (nc.scalar.copy, nc.scalar))):
            cols = slice(g * P, (g + 1) * P)
            y_ps = psum.tile([P, O], F32, name="y_ps%d" % g, tag="bank%d" % g)
            nc.tensor.matmul_mx(
                out=y_ps[:], lhsT=wb_w[:, cols].bitcast(FP8X4), lhsT_scale=wb_s[:, cols],
                rhs=h_c[:].bitcast(FP8X4), rhs_scale=h_s[:], start=True, stop=True,
            )
            y = tile("y%d" % g, [P, O], F32)
            copy(y[:], y_ps[:])
            queue.dma_start(out[cols, :], y[:])
